import numpy as np, ml_dtypes
CORES = [16,17,18,19,150,151]
N = 6
import mx_ref
NC, KT = 256, 2
BF = ml_dtypes.bfloat16
def setup_inputs(rng):
    def f(*shape):
        return mx_ref.flush((rng.standard_normal(shape, dtype=np.float32) * np.exp2(rng.integers(-2, 3, shape[:-1] + (1,)))).astype(BF))
    return {"w": f(N, 128, KT * 512), "x": f(N, 128, KT * 4 * NC)}
def setup_inputs_blocks(rng):
    d = setup_inputs(rng)
    for k in ("w", "x"): d[k] = mx_ref.spread(d[k], rng, 4)
    return d
def setup_inputs_wide(rng):
    d = setup_inputs(rng)
    for k in ("w", "x"): d[k] = mx_ref.flush((d[k].astype(np.float32) * np.exp2(rng.integers(-8, 9, (N, 1, 1))).astype(np.float32)).astype(BF))
    return d
def setup_inputs_zeros(rng):
    d = setup_inputs(rng); v = d["x"].reshape(N, 128, -1, 4).copy()
    v[np.broadcast_to((rng.random((N, 1, v.shape[2], 1)) < 0.33), v.shape)] = 0
    d["x"] = v.reshape(d["x"].shape)
    return d
def reference(w, x):
    QW = [[mx_ref.quantize(w[r][:, 512 * t:512 * t + 512]) for t in range(KT)] for r in range(N)]
    QX = [[mx_ref.quantize(x[j][:, 4 * NC * t:4 * NC * t + 4 * NC]) for t in range(KT)] for j in range(N)]
    y = np.zeros((N, 128, N * NC), np.float32)
    for r in range(N):
        for j in range(N):
            for t in range(KT):
                p = mx_ref.matmul(QW[r][t], QX[j][t])
                y[r][:, NC * j:NC * j + NC] = p if t == 0 else y[r][:, NC * j:NC * j + NC] + p
    return {"y": y}

@@ -1,0 +1,169 @@
+from concourse.bass import DstId, RemoteDMATransfer
+from concourse.mybir import dt, ActivationFunctionType
+
+N, KT, NC, WC = 6, 2, 256, 128
+BANK = 512
+
+SCRATCH = {
+    "xb": ("sbuf", [128, KT * 4 * NC], "bfloat16"),
+    "wb": ("sbuf", [128, KT * 4 * WC], "bfloat16"),
+    "xq": ("sbuf", [128, KT * N * NC], "float8_e4m3fn_x4"),
+    "xs": ("sbuf", [128, KT * N * NC], "uint8"),
+    "wq": ("sbuf", [128, KT * WC], "float8_e4m3fn_x4"),
+    "ws": ("sbuf", [128, KT * WC], "uint8"),
+    "acc": ("psum", [128, BANK * N], "float32"),
+    "yb": ("sbuf", [128, N * NC], "float32"),
+}
+SEMAPHORES = (["ldx%d" % t for t in range(KT)] + ["qx%d" % t for t in range(KT)] + ["ldw", "qw", "sent", "st"]
+              + ["a%d_%d" % (j, t) for j in range(N) for t in range(KT)]
+              + ["mm%d" % j for j in range(N)] + ["ev%d" % j for j in range(N)])
+
+
+def _col(j, t):
+    return (t * N + j) * NC
+
+
+def _count(mask):
+    return bin(mask).count("1")
+
+
+def _plan(cores, topo):
+    groups = []
+    for r, c in enumerate(cores):
+        for grp in groups:
+            h = cores[grp[0]]
+            if topo.host(h) == topo.host(c) and topo.chip(h) == topo.chip(c):
+                grp.append(r)
+                break
+        else:
+            groups.append([r])
+    msgs, landed = [], {}
+    for A in groups:
+        for pos, j in enumerate(A):
+            src = cores[j]
+            peers = [cores[p] for p in A if p != j]
+            for B in groups:
+                if B is A:
+                    continue
+                leave = topo.mask(src, cores[B[0]])
+                stay = topo.mask(src, peers[0]) & ~leave
+                for t in range(KT):
+                    if len(A) >= len(B):
+                        k = (pos // (len(A) // len(B)) + t) % len(B)
+                    else:
+                        k = (t * len(A) + pos) % len(B)
+                    msgs.append(dict(kind="off", src=src, dsts=[cores[B[k]]], t=t, j0=j, nj=1, mask=leave))
+                    msgs.append(dict(kind="on", src=src, dsts=peers, t=t, j0=j, nj=1, mask=stay))
+                    landed.setdefault((B[k], t), []).append(j)
+    for (lander, t), js in sorted(landed.items(), key=lambda kv: (kv[0][1], kv[0][0])):
+        grp = [g_ for g_ in groups if lander in g_][0]
+        others = [cores[p] for p in grp if p != lander]
+        js = sorted(js)
+        while js:
+            n = 1
+            while n < len(js) and js[n] == js[0] + n and (n + 1) * NC * 4 <= 4096:
+                n += 1
+            msgs.append(dict(kind="fwd", src=cores[lander], dsts=others, t=t, j0=js[0], nj=n,
+                             mask=topo.mask(cores[lander], others[0])))
+            js = js[n:]
+    return groups, msgs
+
+
+def rank_program(g, core, T, topo):
+    rank = T.rank_of(core)
+    if rank is None:
+        return
+    cores = list(T.cores)
+    groups, msgs = _plan(cores, topo)
+    mine = [grp for grp in groups if rank in grp][0]
+
+    sem_of, total = {}, {}
+    for m in msgs:
+        if core in m["dsts"]:
+            name = "a%d_%d" % (m["j0"], m["t"])
+            total[name] = total.get(name, 0) + 2 * _count(m["mask"])
+            for j in range(m["j0"], m["j0"] + m["nj"]):
+                sem_of[(j, m["t"])] = name
+    direct = set((m["j0"], m["t"]) for m in msgs if m["kind"] == "off" and core in m["dsts"])
+
+    def wait_chunk(q, j, t):
+        if j == rank:
+            q.wait_ge(T.sem["qx%d" % t], 1)
+        else:
+            q.wait_ge(T.sem[sem_of[(j, t)]], total[sem_of[(j, t)]])
+
+    g.sync.dma_start(T.xb[:, 0:4 * NC], T.x[:, 0:4 * NC]).then_inc(T.sem.ldx0, 16)
+    g.scalar.dma_start(T.xb[:, 4 * NC:8 * NC], T.x[:, 4 * NC:8 * NC]).then_inc(T.sem.ldx1, 16)
+    g.sync.dma_start(T.wb[:], T.w[:]).then_inc(T.sem.ldw, 16)
+
+    for t in range(KT):
+        a = _col(rank, t)
+        g.vector.wait_ge(T.sem["ldx%d" % t], 16)
+        g.vector.quantize_mx(T.xq[:, a:a + NC], T.xs[:, a:a + NC],
+                             T.xb[:, 4 * NC * t:4 * NC * (t + 1)]).then_inc(T.sem["qx%d" % t], 1)
+    g.vector.wait_ge(T.sem.ldw, 16)
+    g.vector.quantize_mx(T.wq[:], T.ws[:], T.wb[:]).then_inc(T.sem.qw, 1)
+
+    sent = [0]
+
+    def call(ms):
+        for plane in (False, True):
+            trs = []
+            for m in ms:
+                a = _col(m["j0"], m["t"])
+                b = a + m["nj"] * NC
+                ap = T.xs[:, a:b] if plane else T.xq[:, a:b].bitcast(dt.uint8)
+                ids = []
+                for d in m["dsts"]:
+                    rid, pid = topo.addr(d, core)
+                    ids.append(DstId(rid=rid, pnc=pid))
+                trs.append(RemoteDMATransfer(dst_ids=ids, dma_engine_mask=m["mask"],
+                                             remote_sem=T.sem["a%d_%d" % (m["j0"], m["t"])],
+                                             srcs=[ap], dsts=[ap for d in m["dsts"]]))
+                sent[0] += _count(m["mask"])
+            g.remote_dma_fused(trs, local_sem=T.sem.sent)
+
+    off = [m for m in msgs if m["src"] == core and m["kind"] == "off"]
+    on = [m for m in msgs if m["src"] == core and m["kind"] == "on"]
+    g.wait_ge(T.sem.qx0, 1)
+    call([off[0]])
+    g.wait_ge(T.sem.qx1, 1)
+    call([off[1], on[0]])
+    call([on[1]])
+    for m in msgs:
+        if m["src"] == core and m["kind"] == "fwd":
+            for j in range(m["j0"], m["j0"] + m["nj"]):
+                wait_chunk(g, j, m["t"])
+            call([m])
+    g.wait_ge(T.sem.sent, sent[0])
+
+    near = [rank] + [p for p in mine if p // 2 == rank // 2 and p != rank] + [p for p in mine if p // 2 != rank // 2]
+    far = [j for j in range(N) if j not in mine]
+    order = [(rank, t) for t in range(KT)] + [(p, t) for t in range(KT) for p in near[1:]]
+    for t in range(KT):
+        order += [(j, t) for j in far if (j, t) in direct] + [(j, t) for j in far if (j, t) not in direct]
+    g.tensor.wait_ge(T.sem.qw, 1)
+    for j, t in order:
+        wait_chunk(g.tensor, j, t)
+        a = _col(j, t)
+        g.tensor.matmul_mx(T.acc[:, BANK * j:BANK * j + NC], T.wq[:, WC * t:WC * (t + 1)], T.ws[:, WC * t:WC * (t + 1)],
+                           T.xq[:, a:a + NC], T.xs[:, a:a + NC], t == 0, t == KT - 1).then_inc(T.sem["mm%d" % j], 1)
+
+    done = [j for j, t in order if t == KT - 1]
+    stores, seen = 0, set()
+    for i, j in enumerate(done):
+        dst, bank = T.yb[:, NC * j:NC * (j + 1)], T.acc[:, BANK * j:BANK * j + NC]
+        if i % 2 == 0:
+            g.vector.wait_ge(T.sem["mm%d" % j], KT)
+            g.vector.tensor_copy(dst, bank).then_inc(T.sem["ev%d" % j], 1)
+        else:
+            g.scalar.wait_ge(T.sem["mm%d" % j], KT)
+            g.scalar.activation(dst, bank, ActivationFunctionType.Copy).then_inc(T.sem["ev%d" % j], 1)
+        seen.add(j)
+        if (j ^ 1) in seen:
+            lo = min(j, j ^ 1)
+            g.sync.wait_ge(T.sem["ev%d" % lo], 1)
+            g.sync.wait_ge(T.sem["ev%d" % (lo + 1)], 1)
+            g.sync.dma_start(T.y[:, NC * lo:NC * (lo + 2)], T.yb[:, NC * lo:NC * (lo + 2)]).then_inc(T.sem.st, 16)
+            stores += 1
+    g.sync.wait_ge(T.sem.st, 16 * stores)

@@ -3,6 +3,7 @@ from concourse.mybir import dt, ActivationFunctionType
 
 N, KT, NC, WC = 6, 2, 256, 128
 BANK = 512
+WORLD = 256
 
 SCRATCH = {
     "xb": ("sbuf", [128, KT * 4 * NC], "bfloat16"),
@@ -15,16 +16,19 @@ SCRATCH = {
     "yb": ("sbuf", [128, N * NC], "float32"),
 }
 SEMAPHORES = (["ldx%d" % t for t in range(KT)] + ["qx%d" % t for t in range(KT)] + ["ldw", "qw", "sent", "st"]
-              + ["a%d_%d" % (j, t) for j in range(N) for t in range(KT)]
+              + ["%s%d_%d" % (k, j, t) for k in "cs" for j in range(N) for t in range(KT)]
               + ["mm%d" % j for j in range(N)] + ["ev%d" % j for j in range(N)])
-
-
-def _col(j, t):
-    return (t * N + j) * NC
 
 
 def _count(mask):
     return bin(mask).count("1")
+
+
+def _col(grp, j, t):
+    if j in grp:
+        return (grp.index(j) * KT + t) * NC
+    far = [p for p in range(N) if p not in grp]
+    return (len(grp) * KT + t * len(far) + far.index(j)) * NC
 
 
 def _plan(cores, topo):
@@ -39,128 +43,162 @@ def _plan(cores, topo):
             groups.append([r])
     msgs, landed = [], {}
     for A in groups:
+        B = [grp for grp in groups if grp is not A][0]
+        idle = [c for c in range(WORLD) if c not in cores and topo.host(c) == topo.host(cores[A[0]])
+                and topo.chip(c) == topo.chip(cores[A[0]]) and topo.die(c) != topo.die(cores[A[0]])]
         for pos, j in enumerate(A):
             src = cores[j]
             peers = [cores[p] for p in A if p != j]
-            for B in groups:
-                if B is A:
-                    continue
-                leave = topo.mask(src, cores[B[0]])
-                stay = topo.mask(src, peers[0]) & ~leave
+            leave = topo.mask(src, cores[B[0]])
+            stay = topo.mask(src, peers[0]) & ~leave
+
+            def off(kind, sender, t, k, wave):
+                msgs.append(dict(kind=kind, src=sender, dsts=[cores[B[k]]], chunks=[(j, t)], a=_col(A, j, t),
+                                 b=_col(B, j, t), mask=topo.mask(sender, cores[B[k]]), eta=2 * wave))
+                landed.setdefault((wave, B[k], t), []).append(j)
+
+            if len(A) <= len(B):
                 for t in range(KT):
-                    if len(A) >= len(B):
-                        k = (pos // (len(A) // len(B)) + t) % len(B)
-                    else:
-                        k = (t * len(A) + pos) % len(B)
-                    msgs.append(dict(kind="off", src=src, dsts=[cores[B[k]]], t=t, j0=j, nj=1, mask=leave))
-                    msgs.append(dict(kind="on", src=src, dsts=peers, t=t, j0=j, nj=1, mask=stay))
-                    landed.setdefault((B[k], t), []).append(j)
-    for (lander, t), js in sorted(landed.items(), key=lambda kv: (kv[0][1], kv[0][0])):
+                    off("off", src, t, (t * len(A) + pos) % len(B), 2 * t)
+            elif pos < len(A) // 2:
+                h = idle[pos]
+                msgs.append(dict(kind="hop", src=src, dsts=[h], chunks=[(j, 0)], a=_col(A, j, 0), b=_col(A, j, 0),
+                                 mask=topo.mask(src, h), eta=0))
+                off("relay", h, 0, pos % len(B), 1)
+                off("off", src, 1, 0, 0)
+            else:
+                off("off", src, 0, 1, 0)
+                off("off", src, 1, pos % len(B), 2)
+            msgs.append(dict(kind="on", src=src, dsts=peers, chunks=[(j, t) for t in range(KT)], a=_col(A, j, 0),
+                             b=_col(A, j, 0), mask=stay, eta=0))
+    for (wave, lander, t), js in sorted(landed.items()):
         grp = [g_ for g_ in groups if lander in g_][0]
+        src = cores[lander]
         others = [cores[p] for p in grp if p != lander]
         js = sorted(js)
         while js:
             n = 1
             while n < len(js) and js[n] == js[0] + n and (n + 1) * NC * 4 <= 4096:
                 n += 1
-            msgs.append(dict(kind="fwd", src=cores[lander], dsts=others, t=t, j0=js[0], nj=n,
-                             mask=topo.mask(cores[lander], others[0])))
+            msgs.append(dict(kind="fwd", src=src, dsts=others, chunks=[(j, t) for j in js[:n]], a=_col(grp, js[0], t),
+                             b=_col(grp, js[0], t), mask=topo.mask(src, others[0]), eta=2 * wave + 1))
             js = js[n:]
     return groups, msgs
 
 
 def rank_program(g, core, T, topo):
     rank = T.rank_of(core)
-    if rank is None:
-        return
     cores = list(T.cores)
     groups, msgs = _plan(cores, topo)
-    mine = [grp for grp in groups if rank in grp][0]
+    if rank is None and not [m for m in msgs if m["src"] == core]:
+        return
 
-    sem_of, total = {}, {}
+    tag_of, total, eta = {}, {}, {}
     for m in msgs:
         if core in m["dsts"]:
-            name = "a%d_%d" % (m["j0"], m["t"])
-            total[name] = total.get(name, 0) + 2 * _count(m["mask"])
-            for j in range(m["j0"], m["j0"] + m["nj"]):
-                sem_of[(j, m["t"])] = name
-    direct = set((m["j0"], m["t"]) for m in msgs if m["kind"] == "off" and core in m["dsts"])
+            tag = "%d_%d" % m["chunks"][0]
+            for k in "cs":
+                total[k + tag] = total.get(k + tag, 0) + _count(m["mask"])
+            for ch in m["chunks"]:
+                tag_of[ch] = tag
+                eta[ch] = m["eta"]
 
-    def wait_chunk(q, j, t):
-        if j == rank:
-            q.wait_ge(T.sem["qx%d" % t], 1)
+    def wait_chunk(q, ch, kinds):
+        if ch[0] == rank:
+            q.wait_ge(T.sem["qx%d" % ch[1]], 1)
         else:
-            q.wait_ge(T.sem[sem_of[(j, t)]], total[sem_of[(j, t)]])
+            for k in kinds:
+                q.wait_ge(T.sem[k + tag_of[ch]], total[k + tag_of[ch]])
+
+    sent = [0]
+
+    def send(m, k):
+        n = len(m["chunks"]) * NC
+        if k == "c":
+            src, dst = T.xq[:, m["a"]:m["a"] + n].bitcast(dt.uint8), T.xq[:, m["b"]:m["b"] + n].bitcast(dt.uint8)
+        else:
+            src, dst = T.xs[:, m["a"]:m["a"] + n], T.xs[:, m["b"]:m["b"] + n]
+        ids = []
+        for d in m["dsts"]:
+            rid, pid = topo.addr(d, core)
+            ids.append(DstId(rid=rid, pnc=pid))
+        g.remote_dma_fused([RemoteDMATransfer(dst_ids=ids, dma_engine_mask=m["mask"],
+                                              remote_sem=T.sem[k + "%d_%d" % m["chunks"][0]],
+                                              srcs=[src], dsts=[dst for d in m["dsts"]])], local_sem=T.sem.sent)
+        sent[0] += _count(m["mask"])
+
+    def pass_on():
+        for m in msgs:
+            if m["src"] == core and m["kind"] in ("relay", "fwd"):
+                for k in "sc":
+                    for ch in m["chunks"]:
+                        wait_chunk(g, ch, k)
+                    send(m, k)
+        g.wait_ge(T.sem.sent, sent[0])
+
+    if rank is None:
+        pass_on()
+        return
+    mine = [grp for grp in groups if rank in grp][0]
 
     g.sync.dma_start(T.xb[:, 0:4 * NC], T.x[:, 0:4 * NC]).then_inc(T.sem.ldx0, 16)
     g.scalar.dma_start(T.xb[:, 4 * NC:8 * NC], T.x[:, 4 * NC:8 * NC]).then_inc(T.sem.ldx1, 16)
     g.sync.dma_start(T.wb[:], T.w[:]).then_inc(T.sem.ldw, 16)
 
     for t in range(KT):
-        a = _col(rank, t)
+        a = _col(mine, rank, t)
         g.vector.wait_ge(T.sem["ldx%d" % t], 16)
         g.vector.quantize_mx(T.xq[:, a:a + NC], T.xs[:, a:a + NC],
                              T.xb[:, 4 * NC * t:4 * NC * (t + 1)]).then_inc(T.sem["qx%d" % t], 1)
     g.vector.wait_ge(T.sem.ldw, 16)
     g.vector.quantize_mx(T.wq[:], T.ws[:], T.wb[:]).then_inc(T.sem.qw, 1)
 
-    sent = [0]
-
-    def call(ms):
-        for plane in (False, True):
-            trs = []
-            for m in ms:
-                a = _col(m["j0"], m["t"])
-                b = a + m["nj"] * NC
-                ap = T.xs[:, a:b] if plane else T.xq[:, a:b].bitcast(dt.uint8)
-                ids = []
-                for d in m["dsts"]:
-                    rid, pid = topo.addr(d, core)
-                    ids.append(DstId(rid=rid, pnc=pid))
-                trs.append(RemoteDMATransfer(dst_ids=ids, dma_engine_mask=m["mask"],
-                                             remote_sem=T.sem["a%d_%d" % (m["j0"], m["t"])],
-                                             srcs=[ap], dsts=[ap for d in m["dsts"]]))
-                sent[0] += _count(m["mask"])
-            g.remote_dma_fused(trs, local_sem=T.sem.sent)
-
-    off = [m for m in msgs if m["src"] == core and m["kind"] == "off"]
-    on = [m for m in msgs if m["src"] == core and m["kind"] == "on"]
+    away = [m for m in msgs if m["src"] == core and m["kind"] in ("hop", "off")]
+    on = [m for m in msgs if m["src"] == core and m["kind"] == "on"][0]
+    early = away[0]["kind"] == "off" and len(on["dsts"]) > 1
     g.wait_ge(T.sem.qx0, 1)
-    call([off[0]])
+    send(away[0], "s")
+    send(away[0], "c")
     g.wait_ge(T.sem.qx1, 1)
-    call([off[1], on[0]])
-    call([on[1]])
-    for m in msgs:
-        if m["src"] == core and m["kind"] == "fwd":
-            for j in range(m["j0"], m["j0"] + m["nj"]):
-                wait_chunk(g, j, m["t"])
-            call([m])
-    g.wait_ge(T.sem.sent, sent[0])
+    if early:
+        send(on, "c")
+    send(away[1], "s")
+    send(away[1], "c")
+    if not early:
+        send(on, "c")
+    send(on, "s")
+    pass_on()
 
     near = [rank] + [p for p in mine if p // 2 == rank // 2 and p != rank] + [p for p in mine if p // 2 != rank // 2]
-    far = [j for j in range(N) if j not in mine]
-    order = [(rank, t) for t in range(KT)] + [(p, t) for t in range(KT) for p in near[1:]]
-    for t in range(KT):
-        order += [(j, t) for j in far if (j, t) in direct] + [(j, t) for j in far if (j, t) not in direct]
+    far = [(j, t) for j in range(N) if j not in mine for t in range(KT)]
+    order = [(p, t) for p in near for t in range(KT)] + sorted(far, key=lambda ch: (eta[ch], ch[0]))
     g.tensor.wait_ge(T.sem.qw, 1)
+    begun, done = set(), []
     for j, t in order:
-        wait_chunk(g.tensor, j, t)
-        a = _col(j, t)
+        wait_chunk(g.tensor, (j, t), "sc")
+        a = _col(mine, j, t)
         g.tensor.matmul_mx(T.acc[:, BANK * j:BANK * j + NC], T.wq[:, WC * t:WC * (t + 1)], T.ws[:, WC * t:WC * (t + 1)],
-                           T.xq[:, a:a + NC], T.xs[:, a:a + NC], t == 0, t == KT - 1).then_inc(T.sem["mm%d" % j], 1)
+                           T.xq[:, a:a + NC], T.xs[:, a:a + NC], j not in begun, j in begun).then_inc(T.sem["mm%d" % j], 1)
+        if j in begun:
+            done.append(j)
+        begun.add(j)
 
-    done = [j for j, t in order if t == KT - 1]
     stores, seen = 0, set()
     for i, j in enumerate(done):
         dst, bank = T.yb[:, NC * j:NC * (j + 1)], T.acc[:, BANK * j:BANK * j + NC]
+        q = g.vector if i % 2 == 0 else g.scalar
+        q.wait_ge(T.sem["mm%d" % j], KT)
         if i % 2 == 0:
-            g.vector.wait_ge(T.sem["mm%d" % j], KT)
-            g.vector.tensor_copy(dst, bank).then_inc(T.sem["ev%d" % j], 1)
+            q.tensor_copy(dst, bank).then_inc(T.sem["ev%d" % j], 1)
         else:
-            g.scalar.wait_ge(T.sem["mm%d" % j], KT)
-            g.scalar.activation(dst, bank, ActivationFunctionType.Copy).then_inc(T.sem["ev%d" % j], 1)
+            q.activation(dst, bank, ActivationFunctionType.Copy).then_inc(T.sem["ev%d" % j], 1)
         seen.add(j)
-        if (j ^ 1) in seen:
+        if i >= len(done) - 2:
+            q = g.sync if i % 2 == 0 else g.scalar
+            q.wait_ge(T.sem["ev%d" % j], 1)
+            q.dma_start(T.y[:, NC * j:NC * (j + 1)], dst).then_inc(T.sem.st, 16)
+            stores += 1
+        elif (j ^ 1) in seen:
             lo = min(j, j ^ 1)
             g.sync.wait_ge(T.sem["ev%d" % lo], 1)
             g.sync.wait_ge(T.sem["ev%d" % (lo + 1)], 1)

from concourse.bass import DstId, RemoteDMATransfer
from concourse.mybir import dt, ActivationFunctionType

N, KT, NC, WC = 6, 2, 256, 128
BANK = 512
WORLD = 256

SCRATCH = {
    "xb": ("sbuf", [128, KT * 4 * NC], "bfloat16"),
    "wb": ("sbuf", [128, KT * 4 * WC], "bfloat16"),
    "xq": ("sbuf", [128, KT * N * NC], "float8_e4m3fn_x4"),
    "xs": ("sbuf", [128, KT * N * NC], "uint8"),
    "wq": ("sbuf", [128, KT * WC], "float8_e4m3fn_x4"),
    "ws": ("sbuf", [128, KT * WC], "uint8"),
    "acc": ("psum", [128, BANK * N], "float32"),
    "yb": ("sbuf", [128, N * NC], "float32"),
}
SEMAPHORES = (["ldx%d" % t for t in range(KT)] + ["qx%d" % t for t in range(KT)] + ["ldw", "qw", "sent", "st"]
              + ["%s%d_%d" % (k, j, t) for k in "cs" for j in range(N) for t in range(KT)]
              + ["mm%d" % j for j in range(N)] + ["ev%d" % j for j in range(N)])


def _count(mask):
    return bin(mask).count("1")


def _col(grp, j, t):
    if j in grp:
        return (grp.index(j) * KT + t) * NC
    far = [p for p in range(N) if p not in grp]
    return (len(grp) * KT + t * len(far) + far.index(j)) * NC


def _plan(cores, topo):
    groups = []
    for r, c in enumerate(cores):
        for grp in groups:
            h = cores[grp[0]]
            if topo.host(h) == topo.host(c) and topo.chip(h) == topo.chip(c):
                grp.append(r)
                break
        else:
            groups.append([r])
    msgs, landed = [], {}
    for A in groups:
        B = [grp for grp in groups if grp is not A][0]
        idle = [c for c in range(WORLD) if c not in cores and topo.host(c) == topo.host(cores[A[0]])
                and topo.chip(c) == topo.chip(cores[A[0]]) and topo.die(c) != topo.die(cores[A[0]])]
        for pos, j in enumerate(A):
            src = cores[j]
            peers = [cores[p] for p in A if p != j]
            leave = topo.mask(src, cores[B[0]])
            stay = topo.mask(src, peers[0]) & ~leave

            def off(kind, sender, t, k, wave):
                msgs.append(dict(kind=kind, src=sender, dsts=[cores[B[k]]], chunks=[(j, t)], a=_col(A, j, t),
                                 b=_col(B, j, t), mask=topo.mask(sender, cores[B[k]]), eta=2 * wave))
                landed.setdefault((wave, B[k], t), []).append(j)

            if len(A) <= len(B):
                for t in range(KT):
                    off("off", src, t, (t * len(A) + pos) % len(B), 2 * t)
            elif pos < len(A) // 2:
                h = idle[pos]
                msgs.append(dict(kind="hop", src=src, dsts=[h], chunks=[(j, 0)], a=_col(A, j, 0), b=_col(A, j, 0),
                                 mask=topo.mask(src, h), eta=0))
                off("relay", h, 0, pos % len(B), 1)
                off("off", src, 1, 0, 0)
            else:
                off("off", src, 0, 1, 0)
                off("off", src, 1, pos % len(B), 2)
            msgs.append(dict(kind="on", src=src, dsts=peers, chunks=[(j, t) for t in range(KT)], a=_col(A, j, 0),
                             b=_col(A, j, 0), mask=stay, eta=0))
    for (wave, lander, t), js in sorted(landed.items()):
        grp = [g_ for g_ in groups if lander in g_][0]
        src = cores[lander]
        others = [cores[p] for p in grp if p != lander]
        js = sorted(js)
        while js:
            n = 1
            while n < len(js) and js[n] == js[0] + n and (n + 1) * NC * 4 <= 4096:
                n += 1
            msgs.append(dict(kind="fwd", src=src, dsts=others, chunks=[(j, t) for j in js[:n]], a=_col(grp, js[0], t),
                             b=_col(grp, js[0], t), mask=topo.mask(src, others[0]), eta=2 * wave + 1))
            js = js[n:]
    return groups, msgs


def rank_program(g, core, T, topo):
    rank = T.rank_of(core)
    cores = list(T.cores)
    groups, msgs = _plan(cores, topo)
    if rank is None and not [m for m in msgs if m["src"] == core]:
        return

    tag_of, total, eta = {}, {}, {}
    for m in msgs:
        if core in m["dsts"]:
            tag = "%d_%d" % m["chunks"][0]
            for k in "cs":
                total[k + tag] = total.get(k + tag, 0) + _count(m["mask"])
            for ch in m["chunks"]:
                tag_of[ch] = tag
                eta[ch] = m["eta"]

    def wait_chunk(q, ch, kinds):
        if ch[0] == rank:
            q.wait_ge(T.sem["qx%d" % ch[1]], 1)
        else:
            for k in kinds:
                q.wait_ge(T.sem[k + tag_of[ch]], total[k + tag_of[ch]])

    sent = [0]

    def send(m, k):
        n = len(m["chunks"]) * NC
        if k == "c":
            src, dst = T.xq[:, m["a"]:m["a"] + n].bitcast(dt.uint8), T.xq[:, m["b"]:m["b"] + n].bitcast(dt.uint8)
        else:
            src, dst = T.xs[:, m["a"]:m["a"] + n], T.xs[:, m["b"]:m["b"] + n]
        ids = []
        for d in m["dsts"]:
            rid, pid = topo.addr(d, core)
            ids.append(DstId(rid=rid, pnc=pid))
        g.remote_dma_fused([RemoteDMATransfer(dst_ids=ids, dma_engine_mask=m["mask"],
                                              remote_sem=T.sem[k + "%d_%d" % m["chunks"][0]],
                                              srcs=[src], dsts=[dst for d in m["dsts"]])], local_sem=T.sem.sent)
        sent[0] += _count(m["mask"])

    def pass_on():
        for m in msgs:
            if m["src"] == core and m["kind"] in ("relay", "fwd"):
                for k in "sc":
                    for ch in m["chunks"]:
                        wait_chunk(g, ch, k)
                    send(m, k)
        g.wait_ge(T.sem.sent, sent[0])

    if rank is None:
        pass_on()
        return
    mine = [grp for grp in groups if rank in grp][0]

    g.sync.dma_start(T.xb[:, 0:4 * NC], T.x[:, 0:4 * NC]).then_inc(T.sem.ldx0, 16)
    g.scalar.dma_start(T.xb[:, 4 * NC:8 * NC], T.x[:, 4 * NC:8 * NC]).then_inc(T.sem.ldx1, 16)
    g.sync.dma_start(T.wb[:], T.w[:]).then_inc(T.sem.ldw, 16)

    for t in range(KT):
        a = _col(mine, rank, t)
        g.vector.wait_ge(T.sem["ldx%d" % t], 16)
        g.vector.quantize_mx(T.xq[:, a:a + NC], T.xs[:, a:a + NC],
                             T.xb[:, 4 * NC * t:4 * NC * (t + 1)]).then_inc(T.sem["qx%d" % t], 1)
    g.vector.wait_ge(T.sem.ldw, 16)
    g.vector.quantize_mx(T.wq[:], T.ws[:], T.wb[:]).then_inc(T.sem.qw, 1)

    away = [m for m in msgs if m["src"] == core and m["kind"] in ("hop", "off")]
    on = [m for m in msgs if m["src"] == core and m["kind"] == "on"][0]
    early = away[0]["kind"] == "off" and len(on["dsts"]) > 1
    g.wait_ge(T.sem.qx0, 1)
    send(away[0], "s")
    send(away[0], "c")
    g.wait_ge(T.sem.qx1, 1)
    if early:
        send(on, "c")
    send(away[1], "s")
    send(away[1], "c")
    if not early:
        send(on, "c")
    send(on, "s")
    pass_on()

    near = [rank] + [p for p in mine if p // 2 == rank // 2 and p != rank] + [p for p in mine if p // 2 != rank // 2]
    far = [(j, t) for j in range(N) if j not in mine for t in range(KT)]
    order = [(p, t) for p in near for t in range(KT)] + sorted(far, key=lambda ch: (eta[ch], ch[0]))
    g.tensor.wait_ge(T.sem.qw, 1)
    begun, done = set(), []
    for j, t in order:
        wait_chunk(g.tensor, (j, t), "sc")
        a = _col(mine, j, t)
        g.tensor.matmul_mx(T.acc[:, BANK * j:BANK * j + NC], T.wq[:, WC * t:WC * (t + 1)], T.ws[:, WC * t:WC * (t + 1)],
                           T.xq[:, a:a + NC], T.xs[:, a:a + NC], j not in begun, j in begun).then_inc(T.sem["mm%d" % j], 1)
        if j in begun:
            done.append(j)
        begun.add(j)

    stores, seen = 0, set()
    for i, j in enumerate(done):
        dst, bank = T.yb[:, NC * j:NC * (j + 1)], T.acc[:, BANK * j:BANK * j + NC]
        q = g.vector if i % 2 == 0 else g.scalar
        q.wait_ge(T.sem["mm%d" % j], KT)
        if i % 2 == 0:
            q.tensor_copy(dst, bank).then_inc(T.sem["ev%d" % j], 1)
        else:
            q.activation(dst, bank, ActivationFunctionType.Copy).then_inc(T.sem["ev%d" % j], 1)
        seen.add(j)
        if i >= len(done) - 2:
            q = g.sync if i % 2 == 0 else g.scalar
            q.wait_ge(T.sem["ev%d" % j], 1)
            q.dma_start(T.y[:, NC * j:NC * (j + 1)], dst).then_inc(T.sem.st, 16)
            stores += 1
        elif (j ^ 1) in seen:
            lo = min(j, j ^ 1)
            g.sync.wait_ge(T.sem["ev%d" % lo], 1)
            g.sync.wait_ge(T.sem["ev%d" % (lo + 1)], 1)
            g.sync.dma_start(T.y[:, NC * lo:NC * (lo + 2)], T.yb[:, NC * lo:NC * (lo + 2)]).then_inc(T.sem.st, 16)
            stores += 1
    g.sync.wait_ge(T.sem.st, 16 * stores)
